import numpy as np
import ml_dtypes


def mxq(x, axis, fmt="e4m3"):
    dtype, down = {"e4m3": (ml_dtypes.float8_e4m3fn, 7), "e5m2": (ml_dtypes.float8_e5m2, 14)}[fmt]
    v = np.moveaxis(np.asarray(x, np.float32).astype(ml_dtypes.bfloat16).astype(np.float64), axis, -1)
    blocks = v.reshape(v.shape[:-1] + (-1, 32))
    amax = np.abs(blocks).max(-1, keepdims=True)
    byte = np.maximum(np.where(amax > 0, np.frexp(amax)[1] - 1 + 127, 0) - down, 1)
    scale = np.exp2(byte - 127.0)
    codes = (blocks / scale).astype(np.float32).astype(dtype).astype(np.float64)
    return np.moveaxis((codes * scale).reshape(v.shape), -1, axis)


WIDE = False


def mx_kscale(k):
    if not WIDE:
        return np.ones(k)
    levels = np.array([10, -10, 5, -5, 0])
    if k % 512:
        return np.exp2(np.random.permutation(np.resize(levels, k // 32))).repeat(32)
    a = np.empty((k // 512, 16))
    for p in range(k // 512):
        a[p, :8] = np.random.permutation(np.resize(levels, 8))
        for g in range(8):
            far = levels[np.abs(levels - a[p, g]) >= 10]
            a[p, g + 8] = far[np.random.randint(len(far))]
    return np.exp2(a.ravel()).repeat(32)


def f64(x):
    return np.asarray(x).astype(np.float64)


def striped(idx):
    return np.tile(idx.reshape(-1, 16).T, (8, 1)).astype(np.uint16)


def unstriped(offs):
    return offs[:16].T.reshape(-1).astype(np.int64)


E2M1 = np.array([0.0, 0.5, 1.0, 1.5, 2.0, 3.0, 4.0, 6.0, -0.0, -0.5, -1.0, -1.5, -2.0, -3.0, -4.0, -6.0])


def pack_weight(w, fmt):
    k, n = w.shape
    w = f64(np.asarray(w, np.float32).astype(ml_dtypes.bfloat16)).reshape(k // 32, 32, n)
    amax = np.abs(w).max(1)
    if fmt == "e4m3":
        byte = np.frexp(amax)[1] - 1 + 127 - 7
    else:
        mant, ex = np.frexp(amax / 6.0)
        byte = np.where(mant > 0.5, ex, ex - 1) + 127
    byte = np.clip(np.where(amax > 0, byte, 1), 1, 254)
    scaled = (w * np.exp2(127.0 - byte)[:, None, :]).reshape(k, n).astype(np.float32)
    by_word = np.ascontiguousarray(scaled.reshape(k // 512, 128, 4, n).transpose(0, 1, 3, 2))
    if fmt == "e4m3":
        words = by_word.astype(ml_dtypes.float8_e4m3fn).view(np.uint8)
    else:
        c = by_word.astype(ml_dtypes.float4_e2m1fn).view(np.uint8) & 0xF
        words = (c[..., 0::2] | (c[..., 1::2] << 4)).reshape(k // 512, 128, 2 * n)
    return np.ascontiguousarray(words), np.ascontiguousarray(byte.astype(np.uint8).reshape(k // 512, 16, n))


def unpack_weight(words, scales, fmt):
    g, _, n = scales.shape
    words = np.ascontiguousarray(words).reshape(g, 128, n, -1)
    if fmt == "e4m3":
        vals = words.view(ml_dtypes.float8_e4m3fn).astype(np.float64)
    else:
        nib = np.empty((g, 128, n, 4), np.uint8)
        nib[..., 0::2] = words & 0xF
        nib[..., 1::2] = words >> 4
        vals = E2M1[nib]
    vals = vals * np.repeat(np.exp2(scales.astype(np.float64) - 127.0), 8, axis=1)[..., None]
    return vals.transpose(0, 1, 3, 2).reshape(g * 512, n)


def gelu(v):
    return 0.5 * v * (1.0 + np.tanh(np.sqrt(2.0 / np.pi) * (v + 0.044715 * v**3)))


K, K2, T, S, P, H, N, T2 = 1024, 512, 2048, 1024, 512, 1024, 512, 2048

def setup_inputs():
    n = np.random.standard_normal
    s, s2, u = mx_kscale(K)[:, None], mx_kscale(K2)[:, None], mx_kscale(H)[:, None]
    tab_words, tab_scales = pack_weight(n((K, T)) * s, "e4m3")
    tab2_words, tab2_scales = pack_weight(n((K2, T)) * s2, "e4m3")
    w2_words, w2_scales = pack_weight(1.1 * n((K2, H)) / np.sqrt(K2) / s2, "e2m1")
    w4_words, w4_scales = pack_weight(1.3 * n((H, N)) / np.sqrt(H) / u, "e2m1")
    perm = np.random.permutation(T2)
    return {
        "tab_words": tab_words, "tab_scales": tab_scales,
        "tab2_words": tab2_words, "tab2_scales": tab2_scales,
        "offs": striped(np.random.permutation(T)[:S]),
        "offs2": striped(np.random.permutation(T)[:P]),
        "pos1": striped(np.random.permutation(S)[:P]),
        "offs3": striped(perm[:S]), "offs4": striped(perm[S:S + P]),
        "w1": (0.54 * n((K, H)) / np.sqrt(K) / s).astype(np.float32),
        "w2_words": w2_words, "w2_scales": w2_scales,
        "w3": (1.1 * n((K2, H)) / np.sqrt(K2) / s2).astype(np.float32),
        "gain": (np.exp(0.3 * n(H)) * u[:, 0]).astype(np.float32),
        "w4_words": w4_words, "w4_scales": w4_scales,
        "w5": (1.5 * n((H, N)) / np.sqrt(H) / u).astype(np.float32),
        "wg1": np.exp(0.3 * n((128, S))).astype(np.float32),
        "wg2": np.exp(0.3 * n((128, P))).astype(np.float32),
        "page1": n((N, T2)).astype(np.float32)}

def reference(tab_words, tab_scales, tab2_words, tab2_scales, offs, offs2, pos1, offs3, offs4, w1, w2_words, w2_scales, w3, gain, w4_words, w4_scales, w5, wg1, wg2, page1):
    v = unpack_weight(tab_words, tab_scales, "e4m3")[:, unstriped(offs)]
    v2 = unpack_weight(tab2_words, tab2_scales, "e4m3")[:, unstriped(offs2)]
    h1 = mxq(f64(w1), 0, "e4m3").T @ v
    h2 = (unpack_weight(w2_words, w2_scales, "e2m1").T @ v2) * (mxq(f64(w3), 0, "e4m3").T @ v2)
    feats = np.concatenate([np.cos(h1), np.tanh(h2 + h1[:, unstriped(pos1)])], axis=1)
    z = mxq(f64(gain)[:, None] * feats, 0, "e4m3")
    y1 = unpack_weight(w4_words, w4_scales, "e2m1").T @ z[:, :S]
    y2 = mxq(f64(w5), 0, "e4m3").T @ z[:, S:]
    out = f64(page1).copy()
    out[:, unstriped(offs3)] = np.tile(f64(wg1), (N // 128, 1)) * y1
    out[:, unstriped(offs4)] = np.tile(f64(wg2), (N // 128, 1)) * y2
    return out

@@ -1,0 +1,355 @@
+from contextlib import ExitStack
+
+import concourse.mybir as mybir
+
+K, K2, T, S, NP, H, N, T2 = 1024, 512, 2048, 1024, 512, 1024, 512, 2048
+FLOPS = 2 * (K * H * S + 2 * K2 * H * NP + H * N * (S + NP))
+
+F32 = mybir.dt.float32
+BF16 = mybir.dt.bfloat16
+I32 = mybir.dt.int32
+U32 = mybir.dt.uint32
+U16 = mybir.dt.uint16
+U8 = mybir.dt.uint8
+FP8X4 = mybir.dt.float8_e4m3fn_x4
+FP4X4 = mybir.dt.float4_e2m1fn_x4
+ACT = mybir.ActivationFunctionType
+ALU = mybir.AluOpType
+
+P = 128
+PACK = 4
+PASS = P * PACK
+CH = 512
+HALF = 256
+AL = 64
+
+
+def tile_list_pallet_buildup_scores_kernel(
+    tc, tab_words, tab_scales, tab2_words, tab2_scales, offs, offs2, pos1, offs3, offs4,
+    w1, w2_words, w2_scales, w3, gain, w4_words, w4_scales, w5, wg1, wg2, page1, out,
+):
+    nc = tc.nc
+    with ExitStack() as ctx:
+        keep = ctx.enter_context(tc.tile_pool(name="keep", bufs=1))
+        ring = ctx.enter_context(tc.tile_pool(name="ring", bufs=1))
+        psum = ctx.enter_context(tc.psum_pool(name="psum", bufs=1))
+
+        def kept(shape, dtype, name):
+            return keep.tile(shape, dtype, name=name, align_bytes=AL)
+
+        def slot(shape, dtype, name, k):
+            return ring.tile(shape, dtype, name=name, tag="slot%d" % k, bufs=1, align_bytes=AL)
+
+        def scratch(shape, dtype, name):
+            return ring.tile(shape, dtype, name=name, tag="scratch", bufs=4, align_bytes=AL)
+
+        def bf16_tile(shape, name):
+            return ring.tile(shape, BF16, name=name, tag="bf16", bufs=5, align_bytes=AL)
+
+        def load_list(src, name):
+            t = keep.tile(list(src.shape), U16, name=name)
+            nc.sync.dma_start(t[:], src)
+            return t
+
+        def load_words(src, name, k):
+            t = slot([P, T], I32, name, k)
+            nc.sync.dma_start(t[:], src.rearrange("p t i -> p (t i)").bitcast(I32))
+            return t
+
+        def load_weight(src, name, k):
+            t = slot([P, PACK, CH], F32, name, k)
+            nc.sync.dma_start(t[:], src.rearrange("(p j) c -> p j c", j=PACK))
+            return t
+
+        def load_page(c, k):
+            t = slot([P, T2], F32, "page%d" % c, k)
+            nc.sync.dma_start(t[:], page1[c * P : (c + 1) * P, :])
+            return t
+
+        def zeroed(shape, name, engine):
+            t = ring.tile(shape, U8, name=name, tag=name, bufs=1, align_bytes=AL)
+            engine.memset(t[:].bitcast(I32), 0)
+            return t
+
+        tab_s = zeroed([P, T], "tab_s", nc.vector)
+        tab2_s = zeroed([P, T], "tab2_s", nc.gpsimd)
+        w2_s_raw = zeroed([P, H], "w2_s_raw", nc.gpsimd)
+        w4_s = zeroed([P, 2 * N], "w4_s", nc.gpsimd)
+
+        raw1 = {}
+        idx = load_list(offs, "idx")
+        raw1[0, 0] = load_weight(w1[0:PASS, 0:CH], "raw1_00", 0)
+        for q in range(4):
+            nc.sync.dma_start(
+                tab_s[32 * q : 32 * q + 8, :].bitcast(I32),
+                tab_scales[:, 4 * q : 4 * q + 4, :].bitcast(I32),
+            )
+        tabw = [load_words(tab_words[0], "tabw0", 1)]
+        raw1[1, 0] = load_weight(w1[PASS:K, 0:CH], "raw1_10", 2)
+        idx2 = load_list(offs2, "idx2")
+        tabw.append(load_words(tab_words[1], "tabw1", 3))
+        for q in range(4):
+            nc.sync.dma_start(
+                tab2_s[32 * q : 32 * q + 4, :].bitcast(I32),
+                tab2_scales[0, 4 * q : 4 * q + 4, :].bitcast(I32),
+            )
+        tab2w = load_words(tab2_words[0], "tab2w", 4)
+        raw3 = [load_weight(w3[:, 0:CH], "raw3_0", 5)]
+        g = kept([P, 2, PACK], F32, "g")
+        nc.sync.dma_start(g[:], gain.rearrange("(b p t) -> p b t", p=P, t=PACK))
+        for q in range(4):
+            nc.sync.dma_start(
+                w2_s_raw[32 * q : 32 * q + 4, :].bitcast(I32),
+                w2_scales[0, 4 * q : 4 * q + 4, :].bitcast(I32),
+            )
+        w2_raw = kept([P, 2 * H], U8, "w2_raw")
+        nc.sync.dma_start(w2_raw[:].bitcast(I32), w2_words[0].bitcast(I32))
+        raw1[0, 1] = load_weight(w1[0:PASS, CH:H], "raw1_01", 6)
+        raw1[1, 1] = load_weight(w1[PASS:K, CH:H], "raw1_11", 7)
+        p1 = load_list(pos1, "p1")
+        raw3.append(load_weight(w3[:, CH:H], "raw3_1", 0))
+        w4_w = kept([P, 2, 2 * N], U8, "w4_w")
+        nc.sync.dma_start(w4_w[:].bitcast(I32), w4_words.rearrange("a p n -> p a n").bitcast(I32))
+        for q in range(4):
+            nc.sync.dma_start(
+                w4_s[32 * q : 32 * q + 4, :].rearrange("r (a n) -> r a n", a=2).bitcast(I32),
+                w4_scales[:, 4 * q : 4 * q + 4, :].rearrange("a r n -> r a n").bitcast(I32),
+            )
+        idx3 = load_list(offs3, "idx3")
+        wg1_sb = kept([P, S], F32, "wg1_sb")
+        nc.sync.dma_start(wg1_sb[:], wg1)
+        page = [load_page(c, 1 + c) for c in range(N // P)]
+        idx4 = load_list(offs4, "idx4")
+        wg2_sb = kept([P, NP], F32, "wg2_sb")
+        nc.sync.dma_start(wg2_sb[:], wg2)
+        raw5 = [load_weight(w5[0:PASS, :], "raw5_0", 7), load_weight(w5[PASS:H, :], "raw5_1", 0)]
+
+        def copy_on(engine, dst, src):
+            if engine == "vector":
+                nc.vector.tensor_copy(dst, src)
+            else:
+                nc.scalar.copy(dst, src)
+
+        def quantise(src, width, name):
+            codes = kept([P, width], U32, name + "_c")
+            scales = kept([P, width], U8, name + "_s")
+            nc.vector.quantize_mx(out=codes[:].bitcast(FP8X4), scales=scales[:], in_=src)
+            return codes, scales
+
+        def quantise_dealt(raw, engine, name):
+            grouped = bf16_tile([P, CH * PACK], name + "_g")
+            copy_on(
+                engine,
+                grouped[:].rearrange("p (t m j) -> p m j t", t=PACK, j=PACK),
+                raw[:].rearrange("p j (m t) -> p m j t", t=PACK),
+            )
+            return quantise(grouped[:], CH, name)
+
+        def quantise_plain(raw, engine, name):
+            grouped = bf16_tile([P, CH * PACK], name + "_g")
+            copy_on(
+                engine,
+                grouped[:].rearrange("p (c i j) -> p c j i", i=4, j=PACK),
+                raw[:].rearrange("p j (c i) -> p c j i", i=4),
+            )
+            return quantise(grouped[:], CH, name)
+
+        def gather(window, offsets, dtype, name, tag=None):
+            t = ring.tile([P, CH], dtype, name=name, tag=tag or name, bufs=1, align_bytes=AL)
+            nc.vector.tensor_copy(t[:], window.indirect(offsets))
+            return t
+
+        def cols16(lst, start, count):
+            return lst[:, start // 16 : (start + count) // 16]
+
+        def woven(ap):
+            return ap.rearrange("p (c i t) -> p c t i", i=4, t=PACK)
+
+        def planes(ap):
+            return ap.rearrange("p t (c i) -> p c t i", i=4)
+
+        def gain_rows(tile, b, width):
+            return tile[:, b : b + 1, :].to_broadcast([P, width, PACK])
+
+        def words(ap):
+            return ap.rearrange("p (n t) -> p n t", t=PACK)
+
+        v, v_s, q1 = {}, {}, {}
+        for c in range(2):
+            v_s[c] = gather(tab_s[:], cols16(idx, c * CH, CH), U8, "v_s%d" % c)
+        q1[0, 0] = quantise_dealt(raw1[0, 0], "scalar", "w1_00")
+        for c in range(2):
+            v[0, c] = gather(tabw[0][:].bitcast(U32), cols16(idx, c * CH, CH), U32, "v0%d" % c)
+        q1[1, 0] = quantise_dealt(raw1[1, 0], "scalar", "w1_10")
+        for c in range(2):
+            v[1, c] = gather(tabw[1][:].bitcast(U32), cols16(idx, c * CH, CH), U32, "v1%d" % c)
+
+        h1 = {}
+        for b in range(2):
+            for t in range(PACK):
+                h1[b, t] = kept([P, S], F32, "h1_%d%d" % (b, t))
+
+        def h1_block(b, c):
+            for t in range(PACK):
+                bank = psum.tile([P, CH], F32, name="h_bank", tag="hy", bufs=4)
+                cols = slice(t * P, (t + 1) * P)
+                for a in range(2):
+                    codes, scales = q1[a, b]
+                    nc.tensor.matmul_mx(
+                        out=bank[:], lhsT=codes[:, cols].bitcast(FP8X4), lhsT_scale=scales[:, cols],
+                        rhs=v[a, c][:].bitcast(FP8X4), rhs_scale=v_s[c][4 * a : P, :],
+                        start=(a == 0), stop=(a == 1),
+                    )
+                nc.scalar.copy(h1[b, t][:, c * CH : (c + 1) * CH], bank[:])
+
+        def sines(b, c):
+            s = scratch([P, PACK, CH], F32, "sin")
+            for t in range(PACK):
+                nc.scalar.activation(s[:, t, :], h1[b, t][:, c * CH : (c + 1) * CH], ACT.Sin, scale=0.5)
+            return s
+
+        def z1_by_vector(s, b, c):
+            sq = scratch([P, CH * PACK], F32, "sq")
+            nc.scalar.activation(woven(sq[:]), planes(s[:]), ACT.Square)
+            z = bf16_tile([P, CH * PACK], "z1")
+            nc.vector.scalar_tensor_tensor(words(z[:]), words(sq[:]), -0.5, gain_rows(g2, b, CH), ALU.add, ALU.mult)
+            return quantise(z[:], CH, "z1_%d%d" % (b, c))
+
+        def squares(s):
+            sq = scratch([P, PACK, CH], F32, "sq")
+            nc.scalar.activation(sq[:], s[:], ACT.Square)
+            return sq
+
+        def z1_by_scalar(sq, b, c):
+            zp = bf16_tile([P, PACK, CH], "zp")
+            for t in range(PACK):
+                nc.scalar.activation(
+                    zp[:, t, :], sq[:, t, :], ACT.Identity, bias=g[:, b, t : t + 1], scale=g2[:, b, t : t + 1]
+                )
+            z = bf16_tile([P, CH * PACK], "z1")
+            nc.scalar.copy(woven(z[:]), planes(zp[:]))
+            return quantise(z[:], CH, "z1_%d%d" % (b, c))
+
+        def y1_tile(c, n, z):
+            bank = psum.tile([P, CH], F32, name="y_bank", tag="hy", bufs=4)
+            for b in (1, 0):
+                nc.tensor.matmul_mx(
+                    out=bank[:], lhsT=w4_w[:, b, 2 * n * P : 2 * (n + 1) * P].bitcast(FP4X4),
+                    lhsT_scale=w4_s[:, b * N + n * P : b * N + (n + 1) * P],
+                    rhs=z[b][0][:].bitcast(FP8X4), rhs_scale=z[b][1][:],
+                    start=(b == 1), stop=(b == 0),
+                )
+            y = ring.tile([P, CH], F32, name="y", tag="y", bufs=4)
+            nc.scalar.copy(y[:], bank[:])
+            nc.vector.tensor_tensor(
+                page[n][:].indirect(cols16(idx3, c * CH, CH)), y[:], wg1_sb[:, c * CH : (c + 1) * CH], ALU.mult
+            )
+
+        def pallet_pair(b, t0, q3, total):
+            h2 = []
+            for t in (t0, t0 + 1):
+                col = b * CH + t * P
+                cols = slice(t * P, (t + 1) * P)
+                bank_a = psum.tile([P, NP], F32, name="bank_a", tag="a", bufs=2)
+                nc.tensor.matmul_mx(
+                    out=bank_a[:], lhsT=w2_w[:, 2 * col : 2 * (col + P)].bitcast(FP4X4),
+                    lhsT_scale=w2_s[:, col : col + P],
+                    rhs=v2[:].bitcast(FP8X4), rhs_scale=v2_s[:], start=True, stop=True,
+                )
+                bank_b = psum.tile([P, NP], F32, name="bank_b", tag="b", bufs=2)
+                nc.tensor.matmul_mx(
+                    out=bank_b[:], lhsT=q3[0][:, cols].bitcast(FP8X4), lhsT_scale=q3[1][:, cols],
+                    rhs=v2[:].bitcast(FP8X4), rhs_scale=v2_s[:], start=True, stop=True,
+                )
+                first = ring.tile([P, NP], F32, name="first", tag="first", bufs=4)
+                nc.scalar.copy(first[:], bank_a[:])
+                prod = ring.tile([P, NP], F32, name="prod", tag="prod", bufs=2)
+                nc.vector.tensor_tensor(prod[:], bank_b[:], first[:], ALU.mult)
+                h2.append(prod)
+            for i, t in enumerate((t0, t0 + 1)):
+                nc.vector.tensor_tensor(total[:, t, :], h1[b, t][:].indirect(p1[:]), h2[i][:], ALU.add)
+
+        def z2_by_scalar(total, b, hf):
+            th = scratch([P, PACK, HALF], F32, "th")
+            nc.scalar.activation(th[:], total[:, :, hf * HALF : (hf + 1) * HALF], ACT.Tanh)
+            zp = bf16_tile([P, PACK, HALF], "zp2")
+            for t in range(PACK):
+                nc.scalar.activation(zp[:, t, :], th[:, t, :], ACT.Copy, scale=g[:, b, t : t + 1])
+            z = bf16_tile([P, HALF * PACK], "z2")
+            nc.scalar.copy(woven(z[:]), planes(zp[:]))
+            return quantise(z[:], HALF, "z2_%d%d" % (b, hf))
+
+        def y2_pair(pieces):
+            bank = psum.tile([P, 2, HALF], F32, name="y2_bank", tag="hy", bufs=4)
+            for i, (hf, n) in enumerate(pieces):
+                cols = slice(n * P, (n + 1) * P)
+                for b in (1, 0):
+                    nc.tensor.matmul_mx(
+                        out=bank[:, i, :], lhsT=q5[b][0][:, cols].bitcast(FP8X4), lhsT_scale=q5[b][1][:, cols],
+                        rhs=z2[b, hf][0][:].bitcast(FP8X4), rhs_scale=z2[b, hf][1][:],
+                        start=(b == 1), stop=(b == 0),
+                    )
+            y = ring.tile([P, 2, HALF], F32, name="y2", tag="y", bufs=4)
+            nc.scalar.copy(y[:], bank[:])
+            for i, (hf, n) in enumerate(pieces):
+                nc.vector.tensor_tensor(
+                    page[n][:].indirect(cols16(idx4, hf * HALF, HALF)), y[:, i, :],
+                    wg2_sb[:, hf * HALF : (hf + 1) * HALF], ALU.mult,
+                )
+                if hf == 1:
+                    nc.sync.dma_start(out[n * P : (n + 1) * P, :], page[n][:])
+
+        h1_block(0, 0)
+        h1_block(0, 1)
+        v2_s = gather(tab2_s[:], idx2[:], U8, "v2_s")
+        v2 = gather(tab2w[:].bitcast(U32), idx2[:], U32, "v2")
+        q3 = [quantise_dealt(raw3[0], "vector", "w3_0")]
+        g2 = kept([P, 2, PACK], F32, "g2")
+        nc.vector.tensor_scalar(g2[:], g[:], -2.0, None, ALU.mult)
+        w2_s = kept([P, H], U8, "w2_s")
+        nc.vector.tensor_copy(
+            w2_s[:].rearrange("p (b t m) -> p b m t", b=2, t=PACK),
+            w2_s_raw[:].rearrange("p (b m t) -> p b m t", b=2, t=PACK),
+        )
+        w2_w = kept([P, 2 * H], U8, "w2_w")
+        nc.vector.tensor_copy(
+            w2_w[:].bitcast(U16).rearrange("p (b t m) -> p b m t", b=2, t=PACK),
+            w2_raw[:].bitcast(U16).rearrange("p (b m t) -> p b m t", b=2, t=PACK),
+        )
+        q1[0, 1] = quantise_dealt(raw1[0, 1], "vector", "w1_01")
+        q1[1, 1] = quantise_dealt(raw1[1, 1], "vector", "w1_11")
+        z_c0 = [z1_by_vector(sines(0, 0), 0, 0)]
+        total = [slot([P, PACK, NP], F32, "total0", 5), slot([P, PACK, NP], F32, "total1", 6)]
+        pallet_pair(0, 0, q3[0], total[0])
+
+        h1_block(1, 0)
+        pallet_pair(0, 2, q3[0], total[0])
+        z_c0.append(z1_by_vector(sines(1, 0), 1, 0))
+        h1_block(1, 1)
+        q3.append(quantise_dealt(raw3[1], "scalar", "w3_1"))
+
+        y1_tile(0, 0, z_c0)
+        s = sines(0, 1)
+        pallet_pair(1, 0, q3[1], total[1])
+        sq = squares(s)
+        y1_tile(0, 1, z_c0)
+        z_c1 = [z1_by_scalar(sq, 0, 1)]
+        pallet_pair(1, 2, q3[1], total[1])
+        s = sines(1, 1)
+        y1_tile(0, 2, z_c0)
+        z_c1.append(z1_by_vector(s, 1, 1))
+        y1_tile(0, 3, z_c0)
+
+        q5 = [quantise_plain(raw5[a], "scalar", "w5_%d" % a) for a in range(2)]
+        z2 = {(0, 0): z2_by_scalar(total[0], 0, 0)}
+        y1_tile(1, 0, z_c1)
+        y1_tile(1, 1, z_c1)
+        z2[1, 0] = z2_by_scalar(total[1], 1, 0)
+        y1_tile(1, 2, z_c1)
+        z2[0, 1] = z2_by_scalar(total[0], 0, 1)
+        y1_tile(1, 3, z_c1)
+        y2_pair([(0, 0), (0, 1)])
+        z2[1, 1] = z2_by_scalar(total[1], 1, 1)
+        y2_pair([(1, 0), (0, 2)])
+        y2_pair([(1, 1), (0, 3)])
+        y2_pair([(1, 2), (1, 3)])

@@ -76,38 +76,33 @@ def tile_list_pallet_buildup_scores_kernel(
         w2_s_raw = zeroed([P, H], "w2_s_raw", nc.gpsimd)
         w4_s = zeroed([P, 2 * N], "w4_s", nc.gpsimd)
 
+        warm = kept([P, 1], F32, "warm")
+        nc.gpsimd.memset(warm[:], 0.0)
+        nc.scalar.activation(warm[:], warm[:], ACT.Silu)
+        def load_scale_rows(tile, rows, src_of):
+            for q in range(4):
+                nc.sync.dma_start(tile[32 * q : 32 * q + rows, :].bitcast(I32), src_of(q).bitcast(I32))
+
         raw1 = {}
         idx = load_list(offs, "idx")
-        raw1[0, 0] = load_weight(w1[0:PASS, 0:CH], "raw1_00", 0)
-        for q in range(4):
-            nc.sync.dma_start(
-                tab_s[32 * q : 32 * q + 8, :].bitcast(I32),
-                tab_scales[:, 4 * q : 4 * q + 4, :].bitcast(I32),
-            )
+        load_scale_rows(tab_s, 8, lambda q: tab_scales[:, 4 * q : 4 * q + 4, :])
         tabw = [load_words(tab_words[0], "tabw0", 1)]
-        raw1[1, 0] = load_weight(w1[PASS:K, 0:CH], "raw1_10", 2)
-        idx2 = load_list(offs2, "idx2")
-        tabw.append(load_words(tab_words[1], "tabw1", 3))
-        for q in range(4):
-            nc.sync.dma_start(
-                tab2_s[32 * q : 32 * q + 4, :].bitcast(I32),
-                tab2_scales[0, 4 * q : 4 * q + 4, :].bitcast(I32),
-            )
-        tab2w = load_words(tab2_words[0], "tab2w", 4)
-        raw3 = [load_weight(w3[:, 0:CH], "raw3_0", 5)]
-        g = kept([P, 2, PACK], F32, "g")
-        nc.sync.dma_start(g[:], gain.rearrange("(b p t) -> p b t", p=P, t=PACK))
-        for q in range(4):
-            nc.sync.dma_start(
-                w2_s_raw[32 * q : 32 * q + 4, :].bitcast(I32),
-                w2_scales[0, 4 * q : 4 * q + 4, :].bitcast(I32),
-            )
+        load_scale_rows(w2_s_raw, 4, lambda q: w2_scales[0, 4 * q : 4 * q + 4, :])
         w2_raw = kept([P, 2 * H], U8, "w2_raw")
         nc.sync.dma_start(w2_raw[:].bitcast(I32), w2_words[0].bitcast(I32))
+        raw1[0, 0] = load_weight(w1[0:PASS, 0:CH], "raw1_00", 0)
+        idx2 = load_list(offs2, "idx2")
+        load_scale_rows(tab2_s, 4, lambda q: tab2_scales[0, 4 * q : 4 * q + 4, :])
+        raw1[1, 0] = load_weight(w1[PASS:K, 0:CH], "raw1_10", 2)
+        tabw.append(load_words(tab_words[1], "tabw1", 3))
+        tab2w = load_words(tab2_words[0], "tab2w", 4)
+        raw3 = [load_weight(w3[:, 0:CH], "raw3_0", 5)]
         raw1[0, 1] = load_weight(w1[0:PASS, CH:H], "raw1_01", 6)
         raw1[1, 1] = load_weight(w1[PASS:K, CH:H], "raw1_11", 7)
         p1 = load_list(pos1, "p1")
         raw3.append(load_weight(w3[:, CH:H], "raw3_1", 0))
+        g = kept([P, 2, PACK], F32, "g")
+        nc.sync.dma_start(g[:], gain.rearrange("(b p t) -> p b t", p=P, t=PACK))
         w4_w = kept([P, 2, 2 * N], U8, "w4_w")
         nc.sync.dma_start(w4_w[:].bitcast(I32), w4_words.rearrange("a p n -> p a n").bitcast(I32))
         for q in range(4):
@@ -136,8 +131,9 @@ def tile_list_pallet_buildup_scores_kernel(
             nc.vector.quantize_mx(out=codes[:].bitcast(FP8X4), scales=scales[:], in_=src)
             return codes, scales
 
-        def quantise_dealt(raw, engine, name):
-            grouped = bf16_tile([P, CH * PACK], name + "_g")
+        def quantise_dealt(raw, engine, name, grouped=None):
+            if grouped is None:
+                grouped = bf16_tile([P, CH * PACK], name + "_g")
             copy_on(
                 engine,
                 grouped[:].rearrange("p (t m j) -> p m j t", t=PACK, j=PACK),
@@ -177,9 +173,10 @@ def tile_list_pallet_buildup_scores_kernel(
         v, v_s, q1 = {}, {}, {}
         for c in range(2):
             v_s[c] = gather(tab_s[:], cols16(idx, c * CH, CH), U8, "v_s%d" % c)
-        q1[0, 0] = quantise_dealt(raw1[0, 0], "scalar", "w1_00")
+        q1[0, 0] = quantise_dealt(raw1[0, 0], "vector", "w1_00")
         for c in range(2):
             v[0, c] = gather(tabw[0][:].bitcast(U32), cols16(idx, c * CH, CH), U32, "v0%d" % c)
+        v2_s = gather(tab2_s[:], idx2[:], U8, "v2_s")
         q1[1, 0] = quantise_dealt(raw1[1, 0], "scalar", "w1_10")
         for c in range(2):
             v[1, c] = gather(tabw[1][:].bitcast(U32), cols16(idx, c * CH, CH), U32, "v1%d" % c)
@@ -215,22 +212,30 @@ def tile_list_pallet_buildup_scores_kernel(
             nc.vector.scalar_tensor_tensor(words(z[:]), words(sq[:]), -0.5, gain_rows(g2, b, CH), ALU.add, ALU.mult)
             return quantise(z[:], CH, "z1_%d%d" % (b, c))
 
-        def squares(s):
+        def z1_planes(b, c):
+            s = scratch([P, PACK, CH], F32, "sin")
             sq = scratch([P, PACK, CH], F32, "sq")
-            nc.scalar.activation(sq[:], s[:], ACT.Square)
-            return sq
-
-        def z1_by_scalar(sq, b, c):
             zp = bf16_tile([P, PACK, CH], "zp")
-            for t in range(PACK):
-                nc.scalar.activation(
-                    zp[:, t, :], sq[:, t, :], ACT.Identity, bias=g[:, b, t : t + 1], scale=g2[:, b, t : t + 1]
-                )
-            z = bf16_tile([P, CH * PACK], "z1")
-            nc.scalar.copy(woven(z[:]), planes(zp[:]))
-            return quantise(z[:], CH, "z1_%d%d" % (b, c))
+            for step in range(PACK + 2):
+                t = step
+                if t < PACK:
+                    nc.scalar.activation(s[:, t, :], h1[b, t][:, c * CH : (c + 1) * CH], ACT.Sin, scale=0.5)
+                t = step - 1
+                if 0 <= t < PACK:
+                    nc.scalar.activation(sq[:, t, :], s[:, t, :], ACT.Square)
+                t = step - 2
+                if 0 <= t < PACK:
+                    nc.scalar.activation(
+                        zp[:, t, :], sq[:, t, :], ACT.Identity, bias=g[:, b, t : t + 1], scale=g2[:, b, t : t + 1]
+                    )
+            return zp
 
-        def y1_tile(c, n, z):
+        def weave(zp, width, name):
+            z = bf16_tile([P, width * PACK], "z")
+            nc.scalar.copy(woven(z[:]), planes(zp[:]))
+            return quantise(z[:], width, name)
+
+        def y1_tile(c, n, z, y=None):
             bank = psum.tile([P, CH], F32, name="y_bank", tag="hy", bufs=4)
             for b in (1, 0):
                 nc.tensor.matmul_mx(
@@ -239,10 +244,11 @@ def tile_list_pallet_buildup_scores_kernel(
                     rhs=z[b][0][:].bitcast(FP8X4), rhs_scale=z[b][1][:],
                     start=(b == 1), stop=(b == 0),
                 )
-            y = ring.tile([P, CH], F32, name="y", tag="y", bufs=4)
-            nc.scalar.copy(y[:], bank[:])
+            if y is None:
+                y = ring.tile([P, CH], F32, name="y", tag="y", bufs=4)[:]
+            nc.scalar.copy(y, bank[:])
             nc.vector.tensor_tensor(
-                page[n][:].indirect(cols16(idx3, c * CH, CH)), y[:], wg1_sb[:, c * CH : (c + 1) * CH], ALU.mult
+                page[n][:].indirect(cols16(idx3, c * CH, CH)), y, wg1_sb[:, c * CH : (c + 1) * CH], ALU.mult
             )
 
         def pallet_pair(b, t0, q3, total):
@@ -263,34 +269,55 @@ def tile_list_pallet_buildup_scores_kernel(
                 )
                 first = ring.tile([P, NP], F32, name="first", tag="first", bufs=4)
                 nc.scalar.copy(first[:], bank_a[:])
-                prod = ring.tile([P, NP], F32, name="prod", tag="prod", bufs=2)
-                nc.vector.tensor_tensor(prod[:], bank_b[:], first[:], ALU.mult)
+                prod = shared[:].bitcast(F32)[:, (t - t0) * NP : (t - t0 + 1) * NP]
+                nc.vector.tensor_tensor(prod, bank_b[:], first[:], ALU.mult)
                 h2.append(prod)
             for i, t in enumerate((t0, t0 + 1)):
-                nc.vector.tensor_tensor(total[:, t, :], h1[b, t][:].indirect(p1[:]), h2[i][:], ALU.add)
+                nc.vector.tensor_tensor(total[:, t, :], h1[b, t][:].indirect(p1[:]), h2[i], ALU.add)
 
-        def z2_by_scalar(total, b, hf):
-            th = scratch([P, PACK, HALF], F32, "th")
-            nc.scalar.activation(th[:], total[:, :, hf * HALF : (hf + 1) * HALF], ACT.Tanh)
-            zp = bf16_tile([P, PACK, HALF], "zp2")
-            for t in range(PACK):
-                nc.scalar.activation(zp[:, t, :], th[:, t, :], ACT.Copy, scale=g[:, b, t : t + 1])
-            z = bf16_tile([P, HALF * PACK], "z2")
-            nc.scalar.copy(woven(z[:]), planes(zp[:]))
-            return quantise(z[:], HALF, "z2_%d%d" % (b, hf))
+        def z2_planes(total, b, start, width):
+            th = scratch([P, PACK, width], F32, "th")
+            zp = bf16_tile([P, PACK, width], "zp2")
+            for step in range(PACK + 1):
+                if step < PACK:
+                    nc.scalar.activation(th[:, step, :], total[:, step, start : start + width], ACT.Tanh)
+                if step > 0:
+                    t = step - 1
+                    nc.scalar.activation(zp[:, t, :], th[:, t, :], ACT.Copy, scale=g[:, b, t : t + 1])
+            return th, zp
 
-        def y2_pair(pieces):
-            bank = psum.tile([P, 2, HALF], F32, name="y2_bank", tag="hy", bufs=4)
+        def reused(tile):
+            return tile[:].rearrange("p t n -> p (t n)").bitcast(F32)[:, :CH]
+
+        def round_w5(raw, grouped, quarter, engine):
+            cols = slice(quarter * P, (quarter + 1) * P)
+            copy_on(
+                engine,
+                grouped[:, cols, :].rearrange("p (c i) j -> p c j i", i=4),
+                raw[:, :, cols].rearrange("p j (c i) -> p c j i", i=4),
+            )
+
+        def z2_by_vector(total, b, start, width):
+            th = scratch([P, width * PACK], F32, "th")
+            nc.scalar.activation(woven(th[:]), planes(total[:, :, start : start + width]), ACT.Tanh)
+            z = bf16_tile([P, width * PACK], "z2")
+            nc.vector.tensor_tensor(words(z[:]), words(th[:]), gain_rows(g, b, width), ALU.mult)
+            return quantise(z[:], width, "z2_%d_%d" % (b, start))
+
+        def y2_pair(pieces, y=None):
+            bank = psum.tile([P, len(pieces), HALF], F32, name="y2_bank", tag="hy", bufs=4)
             for i, (hf, n) in enumerate(pieces):
                 cols = slice(n * P, (n + 1) * P)
                 for b in (1, 0):
                     nc.tensor.matmul_mx(
                         out=bank[:, i, :], lhsT=q5[b][0][:, cols].bitcast(FP8X4), lhsT_scale=q5[b][1][:, cols],
-                        rhs=z2[b, hf][0][:].bitcast(FP8X4), rhs_scale=z2[b, hf][1][:],
+                        rhs=z2[b, hf][0].bitcast(FP8X4), rhs_scale=z2[b, hf][1],
                         start=(b == 1), stop=(b == 0),
                     )
-            y = ring.tile([P, 2, HALF], F32, name="y2", tag="y", bufs=4)
-            nc.scalar.copy(y[:], bank[:])
+            if y is None:
+                y = ring.tile([P, CH], F32, name="y2", tag="y", bufs=4)[:]
+            y = y[:, : len(pieces) * HALF].rearrange("p (i n) -> p i n", n=HALF)
+            nc.scalar.copy(y, bank[:])
             for i, (hf, n) in enumerate(pieces):
                 nc.vector.tensor_tensor(
                     page[n][:].indirect(cols16(idx4, hf * HALF, HALF)), y[:, i, :],
@@ -301,7 +328,6 @@ def tile_list_pallet_buildup_scores_kernel(
 
         h1_block(0, 0)
         h1_block(0, 1)
-        v2_s = gather(tab2_s[:], idx2[:], U8, "v2_s")
         v2 = gather(tab2w[:].bitcast(U32), idx2[:], U32, "v2")
         q3 = [quantise_dealt(raw3[0], "vector", "w3_0")]
         g2 = kept([P, 2, PACK], F32, "g2")
@@ -317,39 +343,49 @@ def tile_list_pallet_buildup_scores_kernel(
             w2_raw[:].bitcast(U16).rearrange("p (b m t) -> p b m t", b=2, t=PACK),
         )
         q1[0, 1] = quantise_dealt(raw1[0, 1], "vector", "w1_01")
-        q1[1, 1] = quantise_dealt(raw1[1, 1], "vector", "w1_11")
-        z_c0 = [z1_by_vector(sines(0, 0), 0, 0)]
+        shared = kept([P, CH * PACK], BF16, "shared")
+        q1[1, 1] = quantise_dealt(raw1[1, 1], "vector", "w1_11", shared)
         total = [slot([P, PACK, NP], F32, "total0", 5), slot([P, PACK, NP], F32, "total1", 6)]
         pallet_pair(0, 0, q3[0], total[0])
+        z_c0 = [z1_by_vector(sines(0, 0), 0, 0)]
 
         h1_block(1, 0)
         pallet_pair(0, 2, q3[0], total[0])
+        q3.append(quantise_dealt(raw3[1], "vector", "w3_1"))
         z_c0.append(z1_by_vector(sines(1, 0), 1, 0))
         h1_block(1, 1)
-        q3.append(quantise_dealt(raw3[1], "scalar", "w3_1"))
 
-        y1_tile(0, 0, z_c0)
-        s = sines(0, 1)
         pallet_pair(1, 0, q3[1], total[1])
-        sq = squares(s)
-        y1_tile(0, 1, z_c0)
-        z_c1 = [z1_by_scalar(sq, 0, 1)]
+        zp = z1_planes(0, 1)
+        y1_tile(0, 0, z_c0)
+        z_c1 = [weave(zp, CH, "z1_01")]
+        y1_tile(0, 1, z_c0, reused(zp))
         pallet_pair(1, 2, q3[1], total[1])
-        s = sines(1, 1)
         y1_tile(0, 2, z_c0)
-        z_c1.append(z1_by_vector(s, 1, 1))
-        y1_tile(0, 3, z_c0)
-
-        q5 = [quantise_plain(raw5[a], "scalar", "w5_%d" % a) for a in range(2)]
-        z2 = {(0, 0): z2_by_scalar(total[0], 0, 0)}
+        zp = z1_planes(1, 1)
+        z_c1.append(weave(zp, CH, "z1_11"))
+        y1_tile(0, 3, z_c0, reused(zp))
+        q5 = []
+        for a in range(2):
+            g5 = bf16_tile([P, N, PACK], "g5")
+            for quarter in range(4):
+                round_w5(raw5[a], g5, quarter, "vector" if (a, quarter) in ((1, 2), (1, 3)) else "scalar")
+            q5.append(quantise(g5[:].rearrange("p n j -> p (n j)"), N, "w5_%d" % a))
         y1_tile(1, 0, z_c1)
         y1_tile(1, 1, z_c1)
-        z2[1, 0] = z2_by_scalar(total[1], 1, 0)
-        y1_tile(1, 2, z_c1)
-        z2[0, 1] = z2_by_scalar(total[0], 0, 1)
-        y1_tile(1, 3, z_c1)
-        y2_pair([(0, 0), (0, 1)])
-        z2[1, 1] = z2_by_scalar(total[1], 1, 1)
-        y2_pair([(1, 0), (0, 2)])
-        y2_pair([(1, 1), (0, 3)])
-        y2_pair([(1, 2), (1, 3)])
+        z2 = {}
+        th, zp = z2_planes(total[0], 0, 0, NP)
+        codes, scales = weave(zp, NP, "z2_0")
+        for hf in range(2):
+            z2[0, hf] = (codes[:, hf * HALF : (hf + 1) * HALF], scales[:, hf * HALF : (hf + 1) * HALF])
+        for hf in range(2):
+            y1_tile(1, 2 + hf, z_c1, reused(zp))
+            th, zp = z2_planes(total[1], 1, hf * HALF, HALF)
+            if hf == 1:
+                y2_pair([(0, 0)], th[:, PACK - 1, :])
+            codes, scales = weave(zp, HALF, "z2_1%d" % hf)
+            z2[1, hf] = (codes[:], scales[:])
+        y2_pair([(0, 1), (0, 2)], reused(zp))
+        y2_pair([(1, 0), (1, 1)])
+        y2_pair([(1, 2), (0, 3)])
+        y2_pair([(1, 3)])

@@ -91,10 +91,10 @@ def tile_list_pallet_buildup_scores_kernel(
         w2_raw = kept([P, 2 * H], U8, "w2_raw")
         nc.sync.dma_start(w2_raw[:].bitcast(I32), w2_words[0].bitcast(I32))
         raw1[0, 0] = load_weight(w1[0:PASS, 0:CH], "raw1_00", 0)
-        idx2 = load_list(offs2, "idx2")
         load_scale_rows(tab2_s, 4, lambda q: tab2_scales[0, 4 * q : 4 * q + 4, :])
         raw1[1, 0] = load_weight(w1[PASS:K, 0:CH], "raw1_10", 2)
         tabw.append(load_words(tab_words[1], "tabw1", 3))
+        idx2 = load_list(offs2, "idx2")
         tab2w = load_words(tab2_words[0], "tab2w", 4)
         raw3 = [load_weight(w3[:, 0:CH], "raw3_0", 5)]
         raw1[0, 1] = load_weight(w1[0:PASS, CH:H], "raw1_01", 6)
@@ -177,10 +177,15 @@ def tile_list_pallet_buildup_scores_kernel(
         for c in range(2):
             v[0, c] = gather(tabw[0][:].bitcast(U32), cols16(idx, c * CH, CH), U32, "v0%d" % c)
         v2_s = gather(tab2_s[:], idx2[:], U8, "v2_s")
-        q1[1, 0] = quantise_dealt(raw1[1, 0], "scalar", "w1_10")
         for c in range(2):
             v[1, c] = gather(tabw[1][:].bitcast(U32), cols16(idx, c * CH, CH), U32, "v1%d" % c)
 
+        grouped = bf16_tile([P, CH * PACK], "w1_10_g")
+        dealt = grouped[:].rearrange("p (t m j) -> p m j t", t=PACK, j=PACK)
+        rows = raw1[1, 0][:].rearrange("p j (m t) -> p m j t", t=PACK)
+        nc.vector.tensor_copy(dealt[:, :, :, :2], rows[:, :, :, :2])
+        nc.scalar.copy(dealt[:, :, :, 2:], rows[:, :, :, 2:])
+        q1[1, 0] = quantise(grouped[:], CH, "w1_10")
         h1 = {}
         for b in range(2):
             for t in range(PACK):

@@ -19,9 +19,19 @@ ALU = mybir.AluOpType
 P = 128
 PACK = 4
 PASS = P * PACK
-CH = 512
-HALF = 256
-AL = 64
+COLS = 512
+PART = NP // 2
+QUADRANT = 32
+ROWS = 4
+PER_COLUMN = 16
+LINE = 4
+ALIGN = 64
+SCRATCH_BUFS = 4
+BF16_BUFS = 5
+SUM_BANKS = 4
+Y_BUFS = 4
+FIRST_BUFS = 4
+W5_ON_VECTOR = 2
 
 
 def tile_list_pallet_buildup_scores_kernel(
@@ -35,41 +45,54 @@ def tile_list_pallet_buildup_scores_kernel(
         psum = ctx.enter_context(tc.psum_pool(name="psum", bufs=1))
 
         def kept(shape, dtype, name):
-            return keep.tile(shape, dtype, name=name, align_bytes=AL)
+            return keep.tile(shape, dtype, name=name, align_bytes=ALIGN)
 
-        def slot(shape, dtype, name, k):
-            return ring.tile(shape, dtype, name=name, tag="slot%d" % k, bufs=1, align_bytes=AL)
+        def own(shape, dtype, name):
+            return ring.tile(shape, dtype, name=name, tag=name, bufs=1, align_bytes=ALIGN)
 
-        def scratch(shape, dtype, name):
-            return ring.tile(shape, dtype, name=name, tag="scratch", bufs=4, align_bytes=AL)
+        def in_slot(shape, dtype, name, slot):
+            return ring.tile(shape, dtype, name=name, tag="slot%d" % slot, bufs=1, align_bytes=ALIGN)
+
+        def scratch(shape, name):
+            return ring.tile(shape, F32, name=name, tag="scratch", bufs=SCRATCH_BUFS, align_bytes=ALIGN)
 
         def bf16_tile(shape, name):
-            return ring.tile(shape, BF16, name=name, tag="bf16", bufs=5, align_bytes=AL)
+            return ring.tile(shape, BF16, name=name, tag="bf16", bufs=BF16_BUFS, align_bytes=ALIGN)
 
-        def load_list(src, name):
-            t = keep.tile(list(src.shape), U16, name=name)
-            nc.sync.dma_start(t[:], src)
-            return t
-
-        def load_words(src, name, k):
-            t = slot([P, T], I32, name, k)
-            nc.sync.dma_start(t[:], src.rearrange("p t i -> p (t i)").bitcast(I32))
-            return t
-
-        def load_weight(src, name, k):
-            t = slot([P, PACK, CH], F32, name, k)
-            nc.sync.dma_start(t[:], src.rearrange("(p j) c -> p j c", j=PACK))
-            return t
-
-        def load_page(c, k):
-            t = slot([P, T2], F32, "page%d" % c, k)
-            nc.sync.dma_start(t[:], page1[c * P : (c + 1) * P, :])
-            return t
+        def result_tile(name):
+            return ring.tile([P, COLS], F32, name=name, tag="y", bufs=Y_BUFS)[:]
 
         def zeroed(shape, name, engine):
-            t = ring.tile(shape, U8, name=name, tag=name, bufs=1, align_bytes=AL)
-            engine.memset(t[:].bitcast(I32), 0)
-            return t
+            tile = own(shape, U8, name)
+            engine.memset(tile[:].bitcast(I32), 0)
+            return tile
+
+        def load_list(src, name):
+            tile = keep.tile(list(src.shape), U16, name=name)
+            nc.sync.dma_start(tile[:], src)
+            return tile
+
+        def load_words(src, name, slot):
+            tile = in_slot([P, T], I32, name, slot)
+            nc.sync.dma_start(tile[:], src.rearrange("p t i -> p (t i)").bitcast(I32))
+            return tile
+
+        def load_weight(src, name, slot):
+            tile = in_slot([P, PACK, COLS], F32, name, slot)
+            nc.sync.dma_start(tile[:], src.rearrange("(p j) c -> p j c", j=PACK))
+            return tile
+
+        def load_page(n, slot):
+            tile = in_slot([P, T2], F32, "page%d" % n, slot)
+            nc.sync.dma_start(tile[:], page1[n * P : (n + 1) * P, :])
+            return tile
+
+        def load_scale_rows(tile, scales):
+            passes = scales.shape[0]
+            for q in range(P // QUADRANT):
+                rows = slice(ROWS * q, ROWS * (q + 1))
+                src = scales[:, rows, :] if passes > 1 else scales[0, rows, :]
+                nc.sync.dma_start(tile[QUADRANT * q : QUADRANT * q + ROWS * passes, :].bitcast(I32), src.bitcast(I32))
 
         tab_s = zeroed([P, T], "tab_s", nc.vector)
         tab2_s = zeroed([P, T], "tab2_s", nc.gpsimd)
@@ -79,51 +102,63 @@ def tile_list_pallet_buildup_scores_kernel(
         warm = kept([P, 1], F32, "warm")
         nc.gpsimd.memset(warm[:], 0.0)
         nc.scalar.activation(warm[:], warm[:], ACT.Silu)
-        def load_scale_rows(tile, rows, src_of):
-            for q in range(4):
-                nc.sync.dma_start(tile[32 * q : 32 * q + rows, :].bitcast(I32), src_of(q).bitcast(I32))
 
         raw1 = {}
         idx = load_list(offs, "idx")
-        load_scale_rows(tab_s, 8, lambda q: tab_scales[:, 4 * q : 4 * q + 4, :])
-        tabw = [load_words(tab_words[0], "tabw0", 1)]
-        load_scale_rows(w2_s_raw, 4, lambda q: w2_scales[0, 4 * q : 4 * q + 4, :])
+        load_scale_rows(tab_s, tab_scales)
+        tab_w = [load_words(tab_words[0], "tabw0", 1)]
+        load_scale_rows(w2_s_raw, w2_scales)
+        raw1[0, 0] = load_weight(w1[0:PASS, 0:COLS], "raw1_00", 0)
+        load_scale_rows(tab2_s, tab2_scales)
+        raw1[1, 0] = load_weight(w1[PASS:K, 0:COLS], "raw1_10", 2)
+        tab_w.append(load_words(tab_words[1], "tabw1", 3))
         w2_raw = kept([P, 2 * H], U8, "w2_raw")
         nc.sync.dma_start(w2_raw[:].bitcast(I32), w2_words[0].bitcast(I32))
-        raw1[0, 0] = load_weight(w1[0:PASS, 0:CH], "raw1_00", 0)
-        load_scale_rows(tab2_s, 4, lambda q: tab2_scales[0, 4 * q : 4 * q + 4, :])
-        raw1[1, 0] = load_weight(w1[PASS:K, 0:CH], "raw1_10", 2)
-        tabw.append(load_words(tab_words[1], "tabw1", 3))
         idx2 = load_list(offs2, "idx2")
-        tab2w = load_words(tab2_words[0], "tab2w", 4)
-        raw3 = [load_weight(w3[:, 0:CH], "raw3_0", 5)]
-        raw1[0, 1] = load_weight(w1[0:PASS, CH:H], "raw1_01", 6)
-        raw1[1, 1] = load_weight(w1[PASS:K, CH:H], "raw1_11", 7)
+        tab2_w = load_words(tab2_words[0], "tab2w", 4)
+        raw3 = [load_weight(w3[:, 0:COLS], "raw3_0", 5)]
+        raw1[0, 1] = load_weight(w1[0:PASS, COLS:H], "raw1_01", 6)
+        raw1[1, 1] = load_weight(w1[PASS:K, COLS:H], "raw1_11", 7)
         p1 = load_list(pos1, "p1")
-        raw3.append(load_weight(w3[:, CH:H], "raw3_1", 0))
+        raw3.append(load_weight(w3[:, COLS:H], "raw3_1", 0))
         g = kept([P, 2, PACK], F32, "g")
         nc.sync.dma_start(g[:], gain.rearrange("(b p t) -> p b t", p=P, t=PACK))
         w4_w = kept([P, 2, 2 * N], U8, "w4_w")
         nc.sync.dma_start(w4_w[:].bitcast(I32), w4_words.rearrange("a p n -> p a n").bitcast(I32))
-        for q in range(4):
+        for q in range(P // QUADRANT):
             nc.sync.dma_start(
-                w4_s[32 * q : 32 * q + 4, :].rearrange("r (a n) -> r a n", a=2).bitcast(I32),
-                w4_scales[:, 4 * q : 4 * q + 4, :].rearrange("a r n -> r a n").bitcast(I32),
+                w4_s[QUADRANT * q : QUADRANT * q + ROWS, :].rearrange("r (a n) -> r a n", a=2).bitcast(I32),
+                w4_scales[:, ROWS * q : ROWS * (q + 1), :].rearrange("a r n -> r a n").bitcast(I32),
             )
         idx3 = load_list(offs3, "idx3")
         wg1_sb = kept([P, S], F32, "wg1_sb")
         nc.sync.dma_start(wg1_sb[:], wg1)
-        page = [load_page(c, 1 + c) for c in range(N // P)]
+        page = [load_page(n, 1 + n) for n in range(N // P)]
         idx4 = load_list(offs4, "idx4")
         wg2_sb = kept([P, NP], F32, "wg2_sb")
         nc.sync.dma_start(wg2_sb[:], wg2)
         raw5 = [load_weight(w5[0:PASS, :], "raw5_0", 7), load_weight(w5[PASS:H, :], "raw5_1", 0)]
 
-        def copy_on(engine, dst, src):
-            if engine == "vector":
-                nc.vector.tensor_copy(dst, src)
-            else:
-                nc.scalar.copy(dst, src)
+        def entries(lst, start, count):
+            return lst[:, start // PER_COLUMN : (start + count) // PER_COLUMN]
+
+        def woven(ap):
+            return ap.rearrange("p (c i t) -> p c t i", i=LINE, t=PACK)
+
+        def planes(ap):
+            return ap.rearrange("p t (c i) -> p c t i", i=LINE)
+
+        def by_word(ap):
+            return ap.rearrange("p (n t) -> p n t", t=PACK)
+
+        def dealt_words(rounded):
+            return rounded[:].rearrange("p (t m j) -> p m j t", t=PACK, j=PACK)
+
+        def weight_rows(raw):
+            return raw[:].rearrange("p j (m t) -> p m j t", t=PACK)
+
+        def as_result(tile):
+            return tile[:].rearrange("p t n -> p (t n)").bitcast(F32)[:, :COLS]
 
         def quantise(src, width, name):
             codes = kept([P, width], U32, name + "_c")
@@ -131,210 +166,167 @@ def tile_list_pallet_buildup_scores_kernel(
             nc.vector.quantize_mx(out=codes[:].bitcast(FP8X4), scales=scales[:], in_=src)
             return codes, scales
 
-        def quantise_dealt(raw, engine, name, grouped=None):
-            if grouped is None:
-                grouped = bf16_tile([P, CH * PACK], name + "_g")
-            copy_on(
-                engine,
-                grouped[:].rearrange("p (t m j) -> p m j t", t=PACK, j=PACK),
-                raw[:].rearrange("p j (m t) -> p m j t", t=PACK),
-            )
-            return quantise(grouped[:], CH, name)
+        def quantise_dealt(raw, rounded, name):
+            nc.vector.tensor_copy(dealt_words(rounded), weight_rows(raw))
+            return quantise(rounded[:], COLS, name)
 
-        def quantise_plain(raw, engine, name):
-            grouped = bf16_tile([P, CH * PACK], name + "_g")
-            copy_on(
-                engine,
-                grouped[:].rearrange("p (c i j) -> p c j i", i=4, j=PACK),
-                raw[:].rearrange("p j (c i) -> p c j i", i=4),
-            )
-            return quantise(grouped[:], CH, name)
-
-        def gather(window, offsets, dtype, name, tag=None):
-            t = ring.tile([P, CH], dtype, name=name, tag=tag or name, bufs=1, align_bytes=AL)
-            nc.vector.tensor_copy(t[:], window.indirect(offsets))
-            return t
-
-        def cols16(lst, start, count):
-            return lst[:, start // 16 : (start + count) // 16]
-
-        def woven(ap):
-            return ap.rearrange("p (c i t) -> p c t i", i=4, t=PACK)
-
-        def planes(ap):
-            return ap.rearrange("p t (c i) -> p c t i", i=4)
-
-        def gain_rows(tile, b, width):
-            return tile[:, b : b + 1, :].to_broadcast([P, width, PACK])
-
-        def words(ap):
-            return ap.rearrange("p (n t) -> p n t", t=PACK)
+        def gather(window, offsets, dtype, name):
+            tile = own([P, COLS], dtype, name)
+            nc.vector.tensor_copy(tile[:], window.indirect(offsets))
+            return tile
 
         v, v_s, q1 = {}, {}, {}
         for c in range(2):
-            v_s[c] = gather(tab_s[:], cols16(idx, c * CH, CH), U8, "v_s%d" % c)
-        q1[0, 0] = quantise_dealt(raw1[0, 0], "vector", "w1_00")
+            v_s[c] = gather(tab_s[:], entries(idx, c * COLS, COLS), U8, "v_s%d" % c)
+        q1[0, 0] = quantise_dealt(raw1[0, 0], bf16_tile([P, PASS * PACK], "w1_00_g"), "w1_00")
         for c in range(2):
-            v[0, c] = gather(tabw[0][:].bitcast(U32), cols16(idx, c * CH, CH), U32, "v0%d" % c)
+            v[0, c] = gather(tab_w[0][:].bitcast(U32), entries(idx, c * COLS, COLS), U32, "v0%d" % c)
         v2_s = gather(tab2_s[:], idx2[:], U8, "v2_s")
         for c in range(2):
-            v[1, c] = gather(tabw[1][:].bitcast(U32), cols16(idx, c * CH, CH), U32, "v1%d" % c)
+            v[1, c] = gather(tab_w[1][:].bitcast(U32), entries(idx, c * COLS, COLS), U32, "v1%d" % c)
 
-        grouped = bf16_tile([P, CH * PACK], "w1_10_g")
-        dealt = grouped[:].rearrange("p (t m j) -> p m j t", t=PACK, j=PACK)
-        rows = raw1[1, 0][:].rearrange("p j (m t) -> p m j t", t=PACK)
-        nc.vector.tensor_copy(dealt[:, :, :, :2], rows[:, :, :, :2])
-        nc.scalar.copy(dealt[:, :, :, 2:], rows[:, :, :, 2:])
-        q1[1, 0] = quantise(grouped[:], CH, "w1_10")
-        h1 = {}
-        for b in range(2):
-            for t in range(PACK):
-                h1[b, t] = kept([P, S], F32, "h1_%d%d" % (b, t))
+        rounded = bf16_tile([P, PASS * PACK], "w1_10_g")
+        nc.vector.tensor_copy(dealt_words(rounded)[:, :, :, : PACK // 2], weight_rows(raw1[1, 0])[:, :, :, : PACK // 2])
+        nc.scalar.copy(dealt_words(rounded)[:, :, :, PACK // 2 :], weight_rows(raw1[1, 0])[:, :, :, PACK // 2 :])
+        q1[1, 0] = quantise(rounded[:], COLS, "w1_10")
+
+        h1 = {(b, t): kept([P, S], F32, "h1_%d%d" % (b, t)) for b in range(2) for t in range(PACK)}
 
         def h1_block(b, c):
             for t in range(PACK):
-                bank = psum.tile([P, CH], F32, name="h_bank", tag="hy", bufs=4)
+                bank = psum.tile([P, COLS], F32, name="h_bank", tag="hy", bufs=SUM_BANKS)
                 cols = slice(t * P, (t + 1) * P)
                 for a in range(2):
                     codes, scales = q1[a, b]
                     nc.tensor.matmul_mx(
                         out=bank[:], lhsT=codes[:, cols].bitcast(FP8X4), lhsT_scale=scales[:, cols],
-                        rhs=v[a, c][:].bitcast(FP8X4), rhs_scale=v_s[c][4 * a : P, :],
+                        rhs=v[a, c][:].bitcast(FP8X4), rhs_scale=v_s[c][ROWS * a : P, :],
                         start=(a == 0), stop=(a == 1),
                     )
-                nc.scalar.copy(h1[b, t][:, c * CH : (c + 1) * CH], bank[:])
+                nc.scalar.copy(h1[b, t][:, c * COLS : (c + 1) * COLS], bank[:])
 
-        def sines(b, c):
-            s = scratch([P, PACK, CH], F32, "sin")
+        def half_sine(dst, b, t, c):
+            nc.scalar.activation(dst, h1[b, t][:, c * COLS : (c + 1) * COLS], ACT.Sin, scale=0.5)
+
+        def z1_ending_on_vector(b, c):
+            sines = scratch([P, PACK, COLS], "sin")
             for t in range(PACK):
-                nc.scalar.activation(s[:, t, :], h1[b, t][:, c * CH : (c + 1) * CH], ACT.Sin, scale=0.5)
-            return s
-
-        def z1_by_vector(s, b, c):
-            sq = scratch([P, CH * PACK], F32, "sq")
-            nc.scalar.activation(woven(sq[:]), planes(s[:]), ACT.Square)
-            z = bf16_tile([P, CH * PACK], "z1")
-            nc.vector.scalar_tensor_tensor(words(z[:]), words(sq[:]), -0.5, gain_rows(g2, b, CH), ALU.add, ALU.mult)
-            return quantise(z[:], CH, "z1_%d%d" % (b, c))
+                half_sine(sines[:, t, :], b, t, c)
+            squares = scratch([P, COLS * PACK], "sq")
+            nc.scalar.activation(woven(squares[:]), planes(sines[:]), ACT.Square)
+            z = bf16_tile([P, COLS * PACK], "z1")
+            nc.vector.scalar_tensor_tensor(
+                by_word(z[:]), by_word(squares[:]), -0.5, g2[:, b : b + 1, :].to_broadcast([P, COLS, PACK]),
+                ALU.add, ALU.mult,
+            )
+            return quantise(z[:], COLS, "z1_%d%d" % (b, c))
 
         def z1_planes(b, c):
-            s = scratch([P, PACK, CH], F32, "sin")
-            sq = scratch([P, PACK, CH], F32, "sq")
-            zp = bf16_tile([P, PACK, CH], "zp")
+            sines = scratch([P, PACK, COLS], "sin")
+            squares = scratch([P, PACK, COLS], "sq")
+            zp = bf16_tile([P, PACK, COLS], "zp")
             for step in range(PACK + 2):
-                t = step
-                if t < PACK:
-                    nc.scalar.activation(s[:, t, :], h1[b, t][:, c * CH : (c + 1) * CH], ACT.Sin, scale=0.5)
-                t = step - 1
-                if 0 <= t < PACK:
-                    nc.scalar.activation(sq[:, t, :], s[:, t, :], ACT.Square)
-                t = step - 2
-                if 0 <= t < PACK:
+                if step < PACK:
+                    half_sine(sines[:, step, :], b, step, c)
+                if 1 <= step <= PACK:
+                    nc.scalar.activation(squares[:, step - 1, :], sines[:, step - 1, :], ACT.Square)
+                if step >= 2:
+                    t = step - 2
                     nc.scalar.activation(
-                        zp[:, t, :], sq[:, t, :], ACT.Identity, bias=g[:, b, t : t + 1], scale=g2[:, b, t : t + 1]
+                        zp[:, t, :], squares[:, t, :], ACT.Identity, bias=g[:, b, t : t + 1], scale=g2[:, b, t : t + 1]
                     )
             return zp
+
+        def z2_planes(b, start, width):
+            tanhs = scratch([P, PACK, width], "th")
+            zp = bf16_tile([P, PACK, width], "zp2")
+            for step in range(PACK + 1):
+                if step < PACK:
+                    nc.scalar.activation(tanhs[:, step, :], total[b][:, step, start : start + width], ACT.Tanh)
+                if step >= 1:
+                    t = step - 1
+                    nc.scalar.activation(zp[:, t, :], tanhs[:, t, :], ACT.Copy, scale=g[:, b, t : t + 1])
+            return tanhs, zp
 
         def weave(zp, width, name):
             z = bf16_tile([P, width * PACK], "z")
             nc.scalar.copy(woven(z[:]), planes(zp[:]))
             return quantise(z[:], width, name)
 
-        def y1_tile(c, n, z, y=None):
-            bank = psum.tile([P, CH], F32, name="y_bank", tag="hy", bufs=4)
-            for b in (1, 0):
-                nc.tensor.matmul_mx(
-                    out=bank[:], lhsT=w4_w[:, b, 2 * n * P : 2 * (n + 1) * P].bitcast(FP4X4),
-                    lhsT_scale=w4_s[:, b * N + n * P : b * N + (n + 1) * P],
-                    rhs=z[b][0][:].bitcast(FP8X4), rhs_scale=z[b][1][:],
-                    start=(b == 1), stop=(b == 0),
-                )
-            if y is None:
-                y = ring.tile([P, CH], F32, name="y", tag="y", bufs=4)[:]
-            nc.scalar.copy(y, bank[:])
-            nc.vector.tensor_tensor(
-                page[n][:].indirect(cols16(idx3, c * CH, CH)), y, wg1_sb[:, c * CH : (c + 1) * CH], ALU.mult
-            )
-
-        def pallet_pair(b, t0, q3, total):
-            h2 = []
-            for t in (t0, t0 + 1):
-                col = b * CH + t * P
+        def pallet_pair(b, first_plane):
+            pair = (first_plane, first_plane + 1)
+            for i, t in enumerate(pair):
+                col = b * COLS + t * P
                 cols = slice(t * P, (t + 1) * P)
-                bank_a = psum.tile([P, NP], F32, name="bank_a", tag="a", bufs=2)
+                bank_a = psum.tile([P, NP], F32, name="bank_a", tag="a", bufs=len(pair))
                 nc.tensor.matmul_mx(
                     out=bank_a[:], lhsT=w2_w[:, 2 * col : 2 * (col + P)].bitcast(FP4X4),
                     lhsT_scale=w2_s[:, col : col + P],
                     rhs=v2[:].bitcast(FP8X4), rhs_scale=v2_s[:], start=True, stop=True,
                 )
-                bank_b = psum.tile([P, NP], F32, name="bank_b", tag="b", bufs=2)
+                bank_b = psum.tile([P, NP], F32, name="bank_b", tag="b", bufs=len(pair))
                 nc.tensor.matmul_mx(
-                    out=bank_b[:], lhsT=q3[0][:, cols].bitcast(FP8X4), lhsT_scale=q3[1][:, cols],
+                    out=bank_b[:], lhsT=q3[b][0][:, cols].bitcast(FP8X4), lhsT_scale=q3[b][1][:, cols],
                     rhs=v2[:].bitcast(FP8X4), rhs_scale=v2_s[:], start=True, stop=True,
                 )
-                first = ring.tile([P, NP], F32, name="first", tag="first", bufs=4)
+                first = ring.tile([P, NP], F32, name="first", tag="first", bufs=FIRST_BUFS)
                 nc.scalar.copy(first[:], bank_a[:])
-                prod = shared[:].bitcast(F32)[:, (t - t0) * NP : (t - t0 + 1) * NP]
-                nc.vector.tensor_tensor(prod, bank_b[:], first[:], ALU.mult)
-                h2.append(prod)
-            for i, t in enumerate((t0, t0 + 1)):
-                nc.vector.tensor_tensor(total[:, t, :], h1[b, t][:].indirect(p1[:]), h2[i], ALU.add)
+                nc.vector.tensor_tensor(h2[i], bank_b[:], first[:], ALU.mult)
+            for i, t in enumerate(pair):
+                nc.vector.tensor_tensor(total[b][:, t, :], h1[b, t][:].indirect(p1[:]), h2[i], ALU.add)
 
-        def z2_planes(total, b, start, width):
-            th = scratch([P, PACK, width], F32, "th")
-            zp = bf16_tile([P, PACK, width], "zp2")
-            for step in range(PACK + 1):
-                if step < PACK:
-                    nc.scalar.activation(th[:, step, :], total[:, step, start : start + width], ACT.Tanh)
-                if step > 0:
-                    t = step - 1
-                    nc.scalar.activation(zp[:, t, :], th[:, t, :], ACT.Copy, scale=g[:, b, t : t + 1])
-            return th, zp
-
-        def reused(tile):
-            return tile[:].rearrange("p t n -> p (t n)").bitcast(F32)[:, :CH]
-
-        def round_w5(raw, grouped, quarter, engine):
-            cols = slice(quarter * P, (quarter + 1) * P)
-            copy_on(
-                engine,
-                grouped[:, cols, :].rearrange("p (c i) j -> p c j i", i=4),
-                raw[:, :, cols].rearrange("p j (c i) -> p c j i", i=4),
+        def y1_tile(c, n, y):
+            bank = psum.tile([P, COLS], F32, name="y_bank", tag="hy", bufs=SUM_BANKS)
+            for b in (1, 0):
+                nc.tensor.matmul_mx(
+                    out=bank[:], lhsT=w4_w[:, b, 2 * n * P : 2 * (n + 1) * P].bitcast(FP4X4),
+                    lhsT_scale=w4_s[:, b * N + n * P : b * N + (n + 1) * P],
+                    rhs=z1[b, c][0][:].bitcast(FP8X4), rhs_scale=z1[b, c][1][:],
+                    start=(b == 1), stop=(b == 0),
+                )
+            nc.scalar.copy(y, bank[:])
+            nc.vector.tensor_tensor(
+                page[n][:].indirect(entries(idx3, c * COLS, COLS)), y, wg1_sb[:, c * COLS : (c + 1) * COLS], ALU.mult
             )
 
-        def z2_by_vector(total, b, start, width):
-            th = scratch([P, width * PACK], F32, "th")
-            nc.scalar.activation(woven(th[:]), planes(total[:, :, start : start + width]), ACT.Tanh)
-            z = bf16_tile([P, width * PACK], "z2")
-            nc.vector.tensor_tensor(words(z[:]), words(th[:]), gain_rows(g, b, width), ALU.mult)
-            return quantise(z[:], width, "z2_%d_%d" % (b, start))
-
-        def y2_pair(pieces, y=None):
-            bank = psum.tile([P, len(pieces), HALF], F32, name="y2_bank", tag="hy", bufs=4)
-            for i, (hf, n) in enumerate(pieces):
+        def y2_pieces(pieces, y):
+            bank = psum.tile([P, len(pieces), PART], F32, name="y2_bank", tag="hy", bufs=SUM_BANKS)
+            for i, (part, n) in enumerate(pieces):
                 cols = slice(n * P, (n + 1) * P)
                 for b in (1, 0):
                     nc.tensor.matmul_mx(
                         out=bank[:, i, :], lhsT=q5[b][0][:, cols].bitcast(FP8X4), lhsT_scale=q5[b][1][:, cols],
-                        rhs=z2[b, hf][0].bitcast(FP8X4), rhs_scale=z2[b, hf][1],
+                        rhs=z2[b, part][0].bitcast(FP8X4), rhs_scale=z2[b, part][1],
                         start=(b == 1), stop=(b == 0),
                     )
-            if y is None:
-                y = ring.tile([P, CH], F32, name="y2", tag="y", bufs=4)[:]
-            y = y[:, : len(pieces) * HALF].rearrange("p (i n) -> p i n", n=HALF)
-            nc.scalar.copy(y, bank[:])
-            for i, (hf, n) in enumerate(pieces):
+            side_by_side = y[:, : len(pieces) * PART].rearrange("p (i n) -> p i n", n=PART)
+            nc.scalar.copy(side_by_side, bank[:])
+            for i, (part, n) in enumerate(pieces):
                 nc.vector.tensor_tensor(
-                    page[n][:].indirect(cols16(idx4, hf * HALF, HALF)), y[:, i, :],
-                    wg2_sb[:, hf * HALF : (hf + 1) * HALF], ALU.mult,
+                    page[n][:].indirect(entries(idx4, part * PART, PART)), side_by_side[:, i, :],
+                    wg2_sb[:, part * PART : (part + 1) * PART], ALU.mult,
                 )
-                if hf == 1:
+                if part == 1:
                     nc.sync.dma_start(out[n * P : (n + 1) * P, :], page[n][:])
 
+        def quantise_w5(a):
+            rounded5 = bf16_tile([P, N, PACK], "g5")
+            quarters = N // P
+            for quarter in range(quarters):
+                cols = slice(quarter * P, (quarter + 1) * P)
+                dst = rounded5[:, cols, :].rearrange("p (c i) j -> p c j i", i=LINE)
+                src = raw5[a][:, :, cols].rearrange("p j (c i) -> p c j i", i=LINE)
+                if a == 1 and quarter >= quarters - W5_ON_VECTOR:
+                    nc.vector.tensor_copy(dst, src)
+                else:
+                    nc.scalar.copy(dst, src)
+            return quantise(rounded5[:].rearrange("p n j -> p (n j)"), N, "w5_%d" % a)
+
+        z1, z2 = {}, {}
         h1_block(0, 0)
         h1_block(0, 1)
-        v2 = gather(tab2w[:].bitcast(U32), idx2[:], U32, "v2")
-        q3 = [quantise_dealt(raw3[0], "vector", "w3_0")]
+        v2 = gather(tab2_w[:].bitcast(U32), idx2[:], U32, "v2")
+        q3 = [quantise_dealt(raw3[0], bf16_tile([P, PASS * PACK], "w3_0_g"), "w3_0")]
         g2 = kept([P, 2, PACK], F32, "g2")
         nc.vector.tensor_scalar(g2[:], g[:], -2.0, None, ALU.mult)
         w2_s = kept([P, H], U8, "w2_s")
@@ -347,50 +339,47 @@ def tile_list_pallet_buildup_scores_kernel(
             w2_w[:].bitcast(U16).rearrange("p (b t m) -> p b m t", b=2, t=PACK),
             w2_raw[:].bitcast(U16).rearrange("p (b m t) -> p b m t", b=2, t=PACK),
         )
-        q1[0, 1] = quantise_dealt(raw1[0, 1], "vector", "w1_01")
-        shared = kept([P, CH * PACK], BF16, "shared")
-        q1[1, 1] = quantise_dealt(raw1[1, 1], "vector", "w1_11", shared)
-        total = [slot([P, PACK, NP], F32, "total0", 5), slot([P, PACK, NP], F32, "total1", 6)]
-        pallet_pair(0, 0, q3[0], total[0])
-        z_c0 = [z1_by_vector(sines(0, 0), 0, 0)]
+        q1[0, 1] = quantise_dealt(raw1[0, 1], bf16_tile([P, PASS * PACK], "w1_01_g"), "w1_01")
+        shared = kept([P, PASS * PACK], BF16, "shared")
+        q1[1, 1] = quantise_dealt(raw1[1, 1], shared, "w1_11")
+        h2 = [shared[:].bitcast(F32)[:, i * NP : (i + 1) * NP] for i in range(2)]
+        total = [in_slot([P, PACK, NP], F32, "total%d" % b, 5 + b) for b in range(2)]
+        pallet_pair(0, 0)
+        z1[0, 0] = z1_ending_on_vector(0, 0)
 
         h1_block(1, 0)
-        pallet_pair(0, 2, q3[0], total[0])
-        q3.append(quantise_dealt(raw3[1], "vector", "w3_1"))
-        z_c0.append(z1_by_vector(sines(1, 0), 1, 0))
+        pallet_pair(0, 2)
+        q3.append(quantise_dealt(raw3[1], bf16_tile([P, PASS * PACK], "w3_1_g"), "w3_1"))
+        z1[1, 0] = z1_ending_on_vector(1, 0)
         h1_block(1, 1)
 
-        pallet_pair(1, 0, q3[1], total[1])
+        pallet_pair(1, 0)
         zp = z1_planes(0, 1)
-        y1_tile(0, 0, z_c0)
-        z_c1 = [weave(zp, CH, "z1_01")]
-        y1_tile(0, 1, z_c0, reused(zp))
-        pallet_pair(1, 2, q3[1], total[1])
-        y1_tile(0, 2, z_c0)
+        y1_tile(0, 0, result_tile("y"))
+        z1[0, 1] = weave(zp, COLS, "z1_01")
+        y1_tile(0, 1, as_result(zp))
+        pallet_pair(1, 2)
+        y1_tile(0, 2, result_tile("y"))
         zp = z1_planes(1, 1)
-        z_c1.append(weave(zp, CH, "z1_11"))
-        y1_tile(0, 3, z_c0, reused(zp))
-        q5 = []
-        for a in range(2):
-            g5 = bf16_tile([P, N, PACK], "g5")
-            for quarter in range(4):
-                round_w5(raw5[a], g5, quarter, "vector" if (a, quarter) in ((1, 2), (1, 3)) else "scalar")
-            q5.append(quantise(g5[:].rearrange("p n j -> p (n j)"), N, "w5_%d" % a))
-        y1_tile(1, 0, z_c1)
-        y1_tile(1, 1, z_c1)
-        z2 = {}
-        th, zp = z2_planes(total[0], 0, 0, NP)
+        z1[1, 1] = weave(zp, COLS, "z1_11")
+        y1_tile(0, 3, as_result(zp))
+        q5 = [quantise_w5(a) for a in range(2)]
+
+        y1_tile(1, 0, result_tile("y"))
+        y1_tile(1, 1, result_tile("y"))
+        tanhs, zp = z2_planes(0, 0, NP)
         codes, scales = weave(zp, NP, "z2_0")
-        for hf in range(2):
-            z2[0, hf] = (codes[:, hf * HALF : (hf + 1) * HALF], scales[:, hf * HALF : (hf + 1) * HALF])
-        for hf in range(2):
-            y1_tile(1, 2 + hf, z_c1, reused(zp))
-            th, zp = z2_planes(total[1], 1, hf * HALF, HALF)
-            if hf == 1:
-                y2_pair([(0, 0)], th[:, PACK - 1, :])
-            codes, scales = weave(zp, HALF, "z2_1%d" % hf)
-            z2[1, hf] = (codes[:], scales[:])
-        y2_pair([(0, 1), (0, 2)], reused(zp))
-        y2_pair([(1, 0), (1, 1)])
-        y2_pair([(1, 2), (0, 3)])
-        y2_pair([(1, 3)])
+        for part in range(2):
+            z2[0, part] = (codes[:, part * PART : (part + 1) * PART], scales[:, part * PART : (part + 1) * PART])
+        for part in range(2):
+            y1_tile(1, 2 + part, as_result(zp))
+            tanhs, zp = z2_planes(1, part * PART, PART)
+            if part == 1:
+                y2_pieces([(0, 0)], tanhs[:, PACK - 1, :])
+            codes, scales = weave(zp, PART, "z2_1%d" % part)
+            z2[1, part] = (codes[:], scales[:])
+
+        y2_pieces([(0, 1), (0, 2)], as_result(zp))
+        y2_pieces([(1, 0), (1, 1)], result_tile("y2"))
+        y2_pieces([(1, 2), (0, 3)], result_tile("y2"))
+        y2_pieces([(1, 3)], result_tile("y2"))

from contextlib import ExitStack

import concourse.mybir as mybir

K, K2, T, S, NP, H, N, T2 = 1024, 512, 2048, 1024, 512, 1024, 512, 2048
FLOPS = 2 * (K * H * S + 2 * K2 * H * NP + H * N * (S + NP))

F32 = mybir.dt.float32
BF16 = mybir.dt.bfloat16
I32 = mybir.dt.int32
U32 = mybir.dt.uint32
U16 = mybir.dt.uint16
U8 = mybir.dt.uint8
FP8X4 = mybir.dt.float8_e4m3fn_x4
FP4X4 = mybir.dt.float4_e2m1fn_x4
ACT = mybir.ActivationFunctionType
ALU = mybir.AluOpType

P = 128
PACK = 4
PASS = P * PACK
COLS = 512
PART = NP // 2
QUADRANT = 32
ROWS = 4
PER_COLUMN = 16
LINE = 4
ALIGN = 64
SCRATCH_BUFS = 4
BF16_BUFS = 5
SUM_BANKS = 4
Y_BUFS = 4
FIRST_BUFS = 4
W5_ON_VECTOR = 2


def tile_list_pallet_buildup_scores_kernel(
    tc, tab_words, tab_scales, tab2_words, tab2_scales, offs, offs2, pos1, offs3, offs4,
    w1, w2_words, w2_scales, w3, gain, w4_words, w4_scales, w5, wg1, wg2, page1, out,
):
    nc = tc.nc
    with ExitStack() as ctx:
        keep = ctx.enter_context(tc.tile_pool(name="keep", bufs=1))
        ring = ctx.enter_context(tc.tile_pool(name="ring", bufs=1))
        psum = ctx.enter_context(tc.psum_pool(name="psum", bufs=1))

        def kept(shape, dtype, name):
            return keep.tile(shape, dtype, name=name, align_bytes=ALIGN)

        def own(shape, dtype, name):
            return ring.tile(shape, dtype, name=name, tag=name, bufs=1, align_bytes=ALIGN)

        def in_slot(shape, dtype, name, slot):
            return ring.tile(shape, dtype, name=name, tag="slot%d" % slot, bufs=1, align_bytes=ALIGN)

        def scratch(shape, name):
            return ring.tile(shape, F32, name=name, tag="scratch", bufs=SCRATCH_BUFS, align_bytes=ALIGN)

        def bf16_tile(shape, name):
            return ring.tile(shape, BF16, name=name, tag="bf16", bufs=BF16_BUFS, align_bytes=ALIGN)

        def result_tile(name):
            return ring.tile([P, COLS], F32, name=name, tag="y", bufs=Y_BUFS)[:]

        def zeroed(shape, name, engine):
            tile = own(shape, U8, name)
            engine.memset(tile[:].bitcast(I32), 0)
            return tile

        def load_list(src, name):
            tile = keep.tile(list(src.shape), U16, name=name)
            nc.sync.dma_start(tile[:], src)
            return tile

        def load_words(src, name, slot):
            tile = in_slot([P, T], I32, name, slot)
            nc.sync.dma_start(tile[:], src.rearrange("p t i -> p (t i)").bitcast(I32))
            return tile

        def load_weight(src, name, slot):
            tile = in_slot([P, PACK, COLS], F32, name, slot)
            nc.sync.dma_start(tile[:], src.rearrange("(p j) c -> p j c", j=PACK))
            return tile

        def load_page(n, slot):
            tile = in_slot([P, T2], F32, "page%d" % n, slot)
            nc.sync.dma_start(tile[:], page1[n * P : (n + 1) * P, :])
            return tile

        def load_scale_rows(tile, scales):
            passes = scales.shape[0]
            for q in range(P // QUADRANT):
                rows = slice(ROWS * q, ROWS * (q + 1))
                src = scales[:, rows, :] if passes > 1 else scales[0, rows, :]
                nc.sync.dma_start(tile[QUADRANT * q : QUADRANT * q + ROWS * passes, :].bitcast(I32), src.bitcast(I32))

        tab_s = zeroed([P, T], "tab_s", nc.vector)
        tab2_s = zeroed([P, T], "tab2_s", nc.gpsimd)
        w2_s_raw = zeroed([P, H], "w2_s_raw", nc.gpsimd)
        w4_s = zeroed([P, 2 * N], "w4_s", nc.gpsimd)

        warm = kept([P, 1], F32, "warm")
        nc.gpsimd.memset(warm[:], 0.0)
        nc.scalar.activation(warm[:], warm[:], ACT.Silu)

        raw1 = {}
        idx = load_list(offs, "idx")
        load_scale_rows(tab_s, tab_scales)
        tab_w = [load_words(tab_words[0], "tabw0", 1)]
        load_scale_rows(w2_s_raw, w2_scales)
        raw1[0, 0] = load_weight(w1[0:PASS, 0:COLS], "raw1_00", 0)
        load_scale_rows(tab2_s, tab2_scales)
        raw1[1, 0] = load_weight(w1[PASS:K, 0:COLS], "raw1_10", 2)
        tab_w.append(load_words(tab_words[1], "tabw1", 3))
        w2_raw = kept([P, 2 * H], U8, "w2_raw")
        nc.sync.dma_start(w2_raw[:].bitcast(I32), w2_words[0].bitcast(I32))
        idx2 = load_list(offs2, "idx2")
        tab2_w = load_words(tab2_words[0], "tab2w", 4)
        raw3 = [load_weight(w3[:, 0:COLS], "raw3_0", 5)]
        raw1[0, 1] = load_weight(w1[0:PASS, COLS:H], "raw1_01", 6)
        raw1[1, 1] = load_weight(w1[PASS:K, COLS:H], "raw1_11", 7)
        p1 = load_list(pos1, "p1")
        raw3.append(load_weight(w3[:, COLS:H], "raw3_1", 0))
        g = kept([P, 2, PACK], F32, "g")
        nc.sync.dma_start(g[:], gain.rearrange("(b p t) -> p b t", p=P, t=PACK))
        w4_w = kept([P, 2, 2 * N], U8, "w4_w")
        nc.sync.dma_start(w4_w[:].bitcast(I32), w4_words.rearrange("a p n -> p a n").bitcast(I32))
        for q in range(P // QUADRANT):
            nc.sync.dma_start(
                w4_s[QUADRANT * q : QUADRANT * q + ROWS, :].rearrange("r (a n) -> r a n", a=2).bitcast(I32),
                w4_scales[:, ROWS * q : ROWS * (q + 1), :].rearrange("a r n -> r a n").bitcast(I32),
            )
        idx3 = load_list(offs3, "idx3")
        wg1_sb = kept([P, S], F32, "wg1_sb")
        nc.sync.dma_start(wg1_sb[:], wg1)
        page = [load_page(n, 1 + n) for n in range(N // P)]
        idx4 = load_list(offs4, "idx4")
        wg2_sb = kept([P, NP], F32, "wg2_sb")
        nc.sync.dma_start(wg2_sb[:], wg2)
        raw5 = [load_weight(w5[0:PASS, :], "raw5_0", 7), load_weight(w5[PASS:H, :], "raw5_1", 0)]

        def entries(lst, start, count):
            return lst[:, start // PER_COLUMN : (start + count) // PER_COLUMN]

        def woven(ap):
            return ap.rearrange("p (c i t) -> p c t i", i=LINE, t=PACK)

        def planes(ap):
            return ap.rearrange("p t (c i) -> p c t i", i=LINE)

        def by_word(ap):
            return ap.rearrange("p (n t) -> p n t", t=PACK)

        def dealt_words(rounded):
            return rounded[:].rearrange("p (t m j) -> p m j t", t=PACK, j=PACK)

        def weight_rows(raw):
            return raw[:].rearrange("p j (m t) -> p m j t", t=PACK)

        def as_result(tile):
            return tile[:].rearrange("p t n -> p (t n)").bitcast(F32)[:, :COLS]

        def quantise(src, width, name):
            codes = kept([P, width], U32, name + "_c")
            scales = kept([P, width], U8, name + "_s")
            nc.vector.quantize_mx(out=codes[:].bitcast(FP8X4), scales=scales[:], in_=src)
            return codes, scales

        def quantise_dealt(raw, rounded, name):
            nc.vector.tensor_copy(dealt_words(rounded), weight_rows(raw))
            return quantise(rounded[:], COLS, name)

        def gather(window, offsets, dtype, name):
            tile = own([P, COLS], dtype, name)
            nc.vector.tensor_copy(tile[:], window.indirect(offsets))
            return tile

        v, v_s, q1 = {}, {}, {}
        for c in range(2):
            v_s[c] = gather(tab_s[:], entries(idx, c * COLS, COLS), U8, "v_s%d" % c)
        q1[0, 0] = quantise_dealt(raw1[0, 0], bf16_tile([P, PASS * PACK], "w1_00_g"), "w1_00")
        for c in range(2):
            v[0, c] = gather(tab_w[0][:].bitcast(U32), entries(idx, c * COLS, COLS), U32, "v0%d" % c)
        v2_s = gather(tab2_s[:], idx2[:], U8, "v2_s")
        for c in range(2):
            v[1, c] = gather(tab_w[1][:].bitcast(U32), entries(idx, c * COLS, COLS), U32, "v1%d" % c)

        rounded = bf16_tile([P, PASS * PACK], "w1_10_g")
        nc.vector.tensor_copy(dealt_words(rounded)[:, :, :, : PACK // 2], weight_rows(raw1[1, 0])[:, :, :, : PACK // 2])
        nc.scalar.copy(dealt_words(rounded)[:, :, :, PACK // 2 :], weight_rows(raw1[1, 0])[:, :, :, PACK // 2 :])
        q1[1, 0] = quantise(rounded[:], COLS, "w1_10")

        h1 = {(b, t): kept([P, S], F32, "h1_%d%d" % (b, t)) for b in range(2) for t in range(PACK)}

        def h1_block(b, c):
            for t in range(PACK):
                bank = psum.tile([P, COLS], F32, name="h_bank", tag="hy", bufs=SUM_BANKS)
                cols = slice(t * P, (t + 1) * P)
                for a in range(2):
                    codes, scales = q1[a, b]
                    nc.tensor.matmul_mx(
                        out=bank[:], lhsT=codes[:, cols].bitcast(FP8X4), lhsT_scale=scales[:, cols],
                        rhs=v[a, c][:].bitcast(FP8X4), rhs_scale=v_s[c][ROWS * a : P, :],
                        start=(a == 0), stop=(a == 1),
                    )
                nc.scalar.copy(h1[b, t][:, c * COLS : (c + 1) * COLS], bank[:])

        def half_sine(dst, b, t, c):
            nc.scalar.activation(dst, h1[b, t][:, c * COLS : (c + 1) * COLS], ACT.Sin, scale=0.5)

        def z1_ending_on_vector(b, c):
            sines = scratch([P, PACK, COLS], "sin")
            for t in range(PACK):
                half_sine(sines[:, t, :], b, t, c)
            squares = scratch([P, COLS * PACK], "sq")
            nc.scalar.activation(woven(squares[:]), planes(sines[:]), ACT.Square)
            z = bf16_tile([P, COLS * PACK], "z1")
            nc.vector.scalar_tensor_tensor(
                by_word(z[:]), by_word(squares[:]), -0.5, g2[:, b : b + 1, :].to_broadcast([P, COLS, PACK]),
                ALU.add, ALU.mult,
            )
            return quantise(z[:], COLS, "z1_%d%d" % (b, c))

        def z1_planes(b, c):
            sines = scratch([P, PACK, COLS], "sin")
            squares = scratch([P, PACK, COLS], "sq")
            zp = bf16_tile([P, PACK, COLS], "zp")
            for step in range(PACK + 2):
                if step < PACK:
                    half_sine(sines[:, step, :], b, step, c)
                if 1 <= step <= PACK:
                    nc.scalar.activation(squares[:, step - 1, :], sines[:, step - 1, :], ACT.Square)
                if step >= 2:
                    t = step - 2
                    nc.scalar.activation(
                        zp[:, t, :], squares[:, t, :], ACT.Identity, bias=g[:, b, t : t + 1], scale=g2[:, b, t : t + 1]
                    )
            return zp

        def z2_planes(b, start, width):
            tanhs = scratch([P, PACK, width], "th")
            zp = bf16_tile([P, PACK, width], "zp2")
            for step in range(PACK + 1):
                if step < PACK:
                    nc.scalar.activation(tanhs[:, step, :], total[b][:, step, start : start + width], ACT.Tanh)
                if step >= 1:
                    t = step - 1
                    nc.scalar.activation(zp[:, t, :], tanhs[:, t, :], ACT.Copy, scale=g[:, b, t : t + 1])
            return tanhs, zp

        def weave(zp, width, name):
            z = bf16_tile([P, width * PACK], "z")
            nc.scalar.copy(woven(z[:]), planes(zp[:]))
            return quantise(z[:], width, name)

        def pallet_pair(b, first_plane):
            pair = (first_plane, first_plane + 1)
            for i, t in enumerate(pair):
                col = b * COLS + t * P
                cols = slice(t * P, (t + 1) * P)
                bank_a = psum.tile([P, NP], F32, name="bank_a", tag="a", bufs=len(pair))
                nc.tensor.matmul_mx(
                    out=bank_a[:], lhsT=w2_w[:, 2 * col : 2 * (col + P)].bitcast(FP4X4),
                    lhsT_scale=w2_s[:, col : col + P],
                    rhs=v2[:].bitcast(FP8X4), rhs_scale=v2_s[:], start=True, stop=True,
                )
                bank_b = psum.tile([P, NP], F32, name="bank_b", tag="b", bufs=len(pair))
                nc.tensor.matmul_mx(
                    out=bank_b[:], lhsT=q3[b][0][:, cols].bitcast(FP8X4), lhsT_scale=q3[b][1][:, cols],
                    rhs=v2[:].bitcast(FP8X4), rhs_scale=v2_s[:], start=True, stop=True,
                )
                first = ring.tile([P, NP], F32, name="first", tag="first", bufs=FIRST_BUFS)
                nc.scalar.copy(first[:], bank_a[:])
                nc.vector.tensor_tensor(h2[i], bank_b[:], first[:], ALU.mult)
            for i, t in enumerate(pair):
                nc.vector.tensor_tensor(total[b][:, t, :], h1[b, t][:].indirect(p1[:]), h2[i], ALU.add)

        def y1_tile(c, n, y):
            bank = psum.tile([P, COLS], F32, name="y_bank", tag="hy", bufs=SUM_BANKS)
            for b in (1, 0):
                nc.tensor.matmul_mx(
                    out=bank[:], lhsT=w4_w[:, b, 2 * n * P : 2 * (n + 1) * P].bitcast(FP4X4),
                    lhsT_scale=w4_s[:, b * N + n * P : b * N + (n + 1) * P],
                    rhs=z1[b, c][0][:].bitcast(FP8X4), rhs_scale=z1[b, c][1][:],
                    start=(b == 1), stop=(b == 0),
                )
            nc.scalar.copy(y, bank[:])
            nc.vector.tensor_tensor(
                page[n][:].indirect(entries(idx3, c * COLS, COLS)), y, wg1_sb[:, c * COLS : (c + 1) * COLS], ALU.mult
            )

        def y2_pieces(pieces, y):
            bank = psum.tile([P, len(pieces), PART], F32, name="y2_bank", tag="hy", bufs=SUM_BANKS)
            for i, (part, n) in enumerate(pieces):
                cols = slice(n * P, (n + 1) * P)
                for b in (1, 0):
                    nc.tensor.matmul_mx(
                        out=bank[:, i, :], lhsT=q5[b][0][:, cols].bitcast(FP8X4), lhsT_scale=q5[b][1][:, cols],
                        rhs=z2[b, part][0].bitcast(FP8X4), rhs_scale=z2[b, part][1],
                        start=(b == 1), stop=(b == 0),
                    )
            side_by_side = y[:, : len(pieces) * PART].rearrange("p (i n) -> p i n", n=PART)
            nc.scalar.copy(side_by_side, bank[:])
            for i, (part, n) in enumerate(pieces):
                nc.vector.tensor_tensor(
                    page[n][:].indirect(entries(idx4, part * PART, PART)), side_by_side[:, i, :],
                    wg2_sb[:, part * PART : (part + 1) * PART], ALU.mult,
                )
                if part == 1:
                    nc.sync.dma_start(out[n * P : (n + 1) * P, :], page[n][:])

        def quantise_w5(a):
            rounded5 = bf16_tile([P, N, PACK], "g5")
            quarters = N // P
            for quarter in range(quarters):
                cols = slice(quarter * P, (quarter + 1) * P)
                dst = rounded5[:, cols, :].rearrange("p (c i) j -> p c j i", i=LINE)
                src = raw5[a][:, :, cols].rearrange("p j (c i) -> p c j i", i=LINE)
                if a == 1 and quarter >= quarters - W5_ON_VECTOR:
                    nc.vector.tensor_copy(dst, src)
                else:
                    nc.scalar.copy(dst, src)
            return quantise(rounded5[:].rearrange("p n j -> p (n j)"), N, "w5_%d" % a)

        z1, z2 = {}, {}
        h1_block(0, 0)
        h1_block(0, 1)
        v2 = gather(tab2_w[:].bitcast(U32), idx2[:], U32, "v2")
        q3 = [quantise_dealt(raw3[0], bf16_tile([P, PASS * PACK], "w3_0_g"), "w3_0")]
        g2 = kept([P, 2, PACK], F32, "g2")
        nc.vector.tensor_scalar(g2[:], g[:], -2.0, None, ALU.mult)
        w2_s = kept([P, H], U8, "w2_s")
        nc.vector.tensor_copy(
            w2_s[:].rearrange("p (b t m) -> p b m t", b=2, t=PACK),
            w2_s_raw[:].rearrange("p (b m t) -> p b m t", b=2, t=PACK),
        )
        w2_w = kept([P, 2 * H], U8, "w2_w")
        nc.vector.tensor_copy(
            w2_w[:].bitcast(U16).rearrange("p (b t m) -> p b m t", b=2, t=PACK),
            w2_raw[:].bitcast(U16).rearrange("p (b m t) -> p b m t", b=2, t=PACK),
        )
        q1[0, 1] = quantise_dealt(raw1[0, 1], bf16_tile([P, PASS * PACK], "w1_01_g"), "w1_01")
        shared = kept([P, PASS * PACK], BF16, "shared")
        q1[1, 1] = quantise_dealt(raw1[1, 1], shared, "w1_11")
        h2 = [shared[:].bitcast(F32)[:, i * NP : (i + 1) * NP] for i in range(2)]
        total = [in_slot([P, PACK, NP], F32, "total%d" % b, 5 + b) for b in range(2)]
        pallet_pair(0, 0)
        z1[0, 0] = z1_ending_on_vector(0, 0)

        h1_block(1, 0)
        pallet_pair(0, 2)
        q3.append(quantise_dealt(raw3[1], bf16_tile([P, PASS * PACK], "w3_1_g"), "w3_1"))
        z1[1, 0] = z1_ending_on_vector(1, 0)
        h1_block(1, 1)

        pallet_pair(1, 0)
        zp = z1_planes(0, 1)
        y1_tile(0, 0, result_tile("y"))
        z1[0, 1] = weave(zp, COLS, "z1_01")
        y1_tile(0, 1, as_result(zp))
        pallet_pair(1, 2)
        y1_tile(0, 2, result_tile("y"))
        zp = z1_planes(1, 1)
        z1[1, 1] = weave(zp, COLS, "z1_11")
        y1_tile(0, 3, as_result(zp))
        q5 = [quantise_w5(a) for a in range(2)]

        y1_tile(1, 0, result_tile("y"))
        y1_tile(1, 1, result_tile("y"))
        tanhs, zp = z2_planes(0, 0, NP)
        codes, scales = weave(zp, NP, "z2_0")
        for part in range(2):
            z2[0, part] = (codes[:, part * PART : (part + 1) * PART], scales[:, part * PART : (part + 1) * PART])
        for part in range(2):
            y1_tile(1, 2 + part, as_result(zp))
            tanhs, zp = z2_planes(1, part * PART, PART)
            if part == 1:
                y2_pieces([(0, 0)], tanhs[:, PACK - 1, :])
            codes, scales = weave(zp, PART, "z2_1%d" % part)
            z2[1, part] = (codes[:], scales[:])

        y2_pieces([(0, 1), (0, 2)], as_result(zp))
        y2_pieces([(1, 0), (1, 1)], result_tile("y2"))
        y2_pieces([(1, 2), (0, 3)], result_tile("y2"))
        y2_pieces([(1, 3)], result_tile("y2"))
